import numpy as np
import ml_dtypes


def mxq(x, axis, fmt="e4m3"):
    dtype, down = {"e4m3": (ml_dtypes.float8_e4m3fn, 7), "e5m2": (ml_dtypes.float8_e5m2, 14)}[fmt]
    v = np.moveaxis(np.asarray(x, np.float32).astype(ml_dtypes.bfloat16).astype(np.float64), axis, -1)
    blocks = v.reshape(v.shape[:-1] + (-1, 32))
    amax = np.abs(blocks).max(-1, keepdims=True)
    byte = np.maximum(np.where(amax > 0, np.frexp(amax)[1] - 1 + 127, 0) - down, 1)
    scale = np.exp2(byte - 127.0)
    codes = (blocks / scale).astype(np.float32).astype(dtype).astype(np.float64)
    return np.moveaxis((codes * scale).reshape(v.shape), -1, axis)


WIDE = False


def mx_kscale(k):
    if not WIDE:
        return np.ones(k)
    levels = np.array([10, -10, 5, -5, 0])
    if k % 512:
        return np.exp2(np.random.permutation(np.resize(levels, k // 32))).repeat(32)
    a = np.empty((k // 512, 16))
    for p in range(k // 512):
        a[p, :8] = np.random.permutation(np.resize(levels, 8))
        for g in range(8):
            far = levels[np.abs(levels - a[p, g]) >= 10]
            a[p, g + 8] = far[np.random.randint(len(far))]
    return np.exp2(a.ravel()).repeat(32)


def f64(x):
    return np.asarray(x).astype(np.float64)


def striped(idx):
    return np.tile(idx.reshape(-1, 16).T, (8, 1)).astype(np.uint16)


def unstriped(offs):
    return offs[:16].T.reshape(-1).astype(np.int64)


def pack_weight(w):
    k, n = w.shape
    w = f64(np.asarray(w, np.float32).astype(ml_dtypes.bfloat16)).reshape(k // 32, 32, n)
    amax = np.abs(w).max(1)
    byte = np.clip(np.where(amax > 0, np.frexp(amax)[1] - 1 + 127 - 7, 1), 1, 254)
    scaled = (w * np.exp2(127.0 - byte)[:, None, :]).reshape(k, n).astype(np.float32)
    words = np.ascontiguousarray(scaled.reshape(k // 512, 128, 4, n).transpose(0, 1, 3, 2)).astype(ml_dtypes.float8_e4m3fn).view(np.uint8)
    return words, np.ascontiguousarray(byte.astype(np.uint8).reshape(k // 512, 16, n))


def unpack_weight(words, scales):
    g, p, n, _ = words.shape
    vals = np.ascontiguousarray(words).view(ml_dtypes.float8_e4m3fn).astype(np.float64) * np.repeat(np.exp2(scales.astype(np.float64) - 127.0), 8, axis=1)[..., None]
    return vals.transpose(0, 1, 3, 2).reshape(g * 512, n)


H, K, T, S, N = 512, 512, 2048, 512, 128


def setup_inputs():
    n = np.random.standard_normal
    s = mx_kscale(K)[:, None]
    u = mx_kscale(H)
    packed_xT = pack_weight(n((K, T)) * s)
    packed_eT = pack_weight(n((K, T)) * s)
    return {
        "x_words": packed_xT[0],
        "x_scales": packed_xT[1],
        "e_words": packed_eT[0],
        "e_scales": packed_eT[1],
        "w1": (n((K, H)) / np.sqrt(K) / s).astype(np.float32),
        "unit": (np.random.uniform(0.5, 1.5, (H, 1)) * u[:, None]).astype(np.float32),
        "w2": (n((H, N)) / np.sqrt(H) / u[:, None]).astype(np.float32),
        "skip": (n((N, S))).astype(np.float32),
        "offs": striped(np.random.permutation(T)[:S]),
    }


def reference(x_words, x_scales, e_words, e_scales, w1, unit, w2, skip, offs):
    xq = unpack_weight(x_words, x_scales)[:, unstriped(offs)]
    w1q = mxq(f64(w1), 0, "e4m3")
    hid = np.tanh(w1q.T @ xq)
    slo = -1.0 * ((hid) ** 2) + 1.0
    e_offs = unpack_weight(e_words, e_scales)[:, unstriped(offs)]
    tan = w1q.T @ e_offs
    done = slo * tan
    zone = f64(unit) * done
    return (mxq(f64(w2), 0, "e4m3").T @ mxq(zone, 0, "e4m3")) + f64(skip)

@@ -1,0 +1,183 @@
+from contextlib import ExitStack
+
+import concourse.mybir as mybir
+
+H, K, T, S, N = 512, 512, 2048, 512, 128
+FLOPS = 2 * K * H * S * 2 + 2 * H * N * S
+
+F32 = mybir.dt.float32
+BF16 = mybir.dt.bfloat16
+I32 = mybir.dt.int32
+U32 = mybir.dt.uint32
+U16 = mybir.dt.uint16
+U8 = mybir.dt.uint8
+FP8X4 = mybir.dt.float8_e4m3fn_x4
+ACT = mybir.ActivationFunctionType
+ALU = mybir.AluOpType
+
+P = 128
+PACK = 4
+HALF = S // 2
+CHUNK = 128
+LIST_COLS = HALF // 16
+E_PLANE = 4
+W1_HALF = H // 2
+M_HALF = W1_HALF // PACK
+M_ON_SCALAR = 40
+
+
+def tile_picked_yjvptn_jvp_p_kernel(
+    tc, x_words, x_scales, e_words, e_scales, w1, unit, w2, skip, offs, out
+):
+    nc = tc.nc
+    with ExitStack() as ctx:
+        keep = ctx.enter_context(tc.tile_pool(name="keep", bufs=1))
+        psum = ctx.enter_context(tc.psum_pool(name="psum", bufs=1))
+
+        offsets = keep.tile([P, S // 16], U16, name="offsets")
+        nc.sync.dma_start(offsets[:], offs)
+
+        x_scale_table = keep.tile([P, T], U8, name="x_scale_table", tag="x_scale_then_w1", align_bytes=64)
+        e_scale_table = keep.tile([P, T], U8, name="e_scale_table", tag="e_scale_then_codes", align_bytes=64)
+        nc.vector.memset(x_scale_table[:].bitcast(I32), 0)
+        nc.vector.memset(e_scale_table[:].bitcast(I32), 0)
+
+        warm_in = keep.tile([P, 1], F32, name="warm_in")
+        warm_out = keep.tile([P, 1], F32, name="warm_out")
+        nc.gpsimd.memset(warm_in[:], 0.0)
+        nc.scalar.activation(warm_out[:], warm_in[:], ACT.Tanh)
+
+        def load_scale_rows(table, scales, plane):
+            for r in range(4):
+                nc.sync.dma_start(table[plane + r : P : 32, :].bitcast(I32), scales[0, r:16:4, :].bitcast(I32))
+
+        def load_words(table, words):
+            nc.sync.dma_start(table[:].bitcast(I32), words[0].rearrange("p n t -> p (n t)").bitcast(I32))
+
+        unit_sb = keep.tile([P, PACK], F32, name="unit_sb")
+        nc.sync.dma_start(unit_sb[:], unit.rearrange("(p t) o -> p (t o)", t=PACK))
+        w1_rows = w1.rearrange("(p j) c -> p j c", j=PACK)
+        w1_raw = [keep.tile([P, PACK, W1_HALF], F32, name="w1_raw%d" % a) for a in range(2)]
+        nc.sync.dma_start(w1_raw[0][:], w1_rows[:, :, :W1_HALF])
+        load_scale_rows(x_scale_table, x_scales, 0)
+        nc.sync.dma_start(w1_raw[1][:], w1_rows[:, :, W1_HALF:])
+        x_table = keep.tile([P, T], U32, name="x_table")
+        load_words(x_table, x_words)
+        load_scale_rows(e_scale_table, e_scales, E_PLANE)
+        e_table = keep.tile([P, T], U32, name="e_table", tag="e_then_gain")
+        load_words(e_table, e_words)
+        w2_raw = keep.tile([P, PACK, N], F32, name="w2_raw")
+        nc.sync.dma_start(w2_raw[:], w2.rearrange("(p j) c -> p j c", j=PACK))
+        skip_sb = keep.tile([P, S], F32, name="skip_sb")
+        nc.sync.dma_start(skip_sb[:], skip)
+
+        x_scale = keep.tile([P, S], U8, name="x_scale", align_bytes=64)
+        nc.vector.tensor_copy(x_scale[:], x_scale_table[:].indirect(offsets[:]))
+
+        minus_unit = keep.tile([P, PACK], F32, name="minus_unit")
+        nc.vector.tensor_scalar(minus_unit[:], unit_sb[:], -1.0, None, ALU.mult)
+
+        w1_grouped = keep.tile([P, PACK, P, PACK], BF16, name="w1_grouped", align_bytes=64)
+
+        def deal_w1(copy, a, m0, m1):
+            copy(
+                w1_grouped[:, :, a * M_HALF + m0 : a * M_HALF + m1, :].rearrange("p t m j -> p m j t"),
+                w1_raw[a][:, :, PACK * m0 : PACK * m1].rearrange("p j (m t) -> p m j t", t=PACK),
+            )
+
+        deal_w1(nc.scalar.copy, 0, 0, M_HALF)
+        deal_w1(nc.scalar.copy, 1, 0, M_ON_SCALAR)
+        deal_w1(nc.vector.tensor_copy, 1, M_ON_SCALAR, M_HALF)
+        w1_codes = keep.tile([P, H], U32, name="w1_codes", tag="x_scale_then_w1", align_bytes=64)
+        w1_scale = keep.tile([P, H], U8, name="w1_scale", align_bytes=64)
+        nc.vector.quantize_mx(w1_codes[:].bitcast(FP8X4), w1_scale[:], w1_grouped[:].rearrange("p t m j -> p (t m j)"))
+
+        def first_product(bank, t, codes, scale):
+            cols = slice(t * P, (t + 1) * P)
+            nc.tensor.matmul_mx(
+                bank, lhsT=w1_codes[:, cols].bitcast(FP8X4), lhsT_scale=w1_scale[:, cols],
+                rhs=codes.bitcast(FP8X4), rhs_scale=scale, start=True, stop=True,
+            )
+
+        def list_half(half):
+            return offsets[:, half * LIST_COLS : (half + 1) * LIST_COLS]
+
+        squares = []
+        for half in range(2):
+            x_codes = keep.tile([P, HALF], U32, name="x_codes%d" % half, align_bytes=64)
+            nc.vector.tensor_copy(x_codes[:], x_table[:].indirect(list_half(half)))
+            for pair in range(2):
+                pre = psum.tile([P, 2, HALF], F32, name="pre", tag="bank%d" % (2 * half + pair))
+                for i in range(2):
+                    first_product(pre[:, i, :], 2 * pair + i, x_codes[:], x_scale[:, half * HALF : (half + 1) * HALF])
+                hid = keep.tile([P, 2, HALF], F32, name="hid", bufs=2)
+                nc.scalar.activation(hid[:], pre[:], ACT.Tanh)
+                square = keep.tile([P, 2, HALF], F32, name="square%d%d" % (half, pair))
+                nc.scalar.activation(square[:], hid[:], ACT.Square)
+                squares.append(square)
+
+        e_scale = keep.tile([P, S], U8, name="e_scale", align_bytes=64)
+        nc.vector.tensor_copy(e_scale[:], e_scale_table[:].indirect(offsets[:]))
+
+        tans = []
+        for half in range(2):
+            e_codes = keep.tile(
+                [P, HALF], U32, name="e_codes", tag="e_scale_then_codes" if half == 0 else "e_codes", align_bytes=64
+            )
+            nc.vector.tensor_copy(e_codes[:], e_table[:].indirect(list_half(half)))
+            for part in range(2):
+                c = 2 * half + part
+                tan = psum.tile([P, PACK, CHUNK], F32, name="tan", tag="bank%d" % (4 + c))
+                for t in range(PACK):
+                    first_product(
+                        tan[:, t, :], t, e_codes[:, part * CHUNK : (part + 1) * CHUNK],
+                        e_scale[E_PLANE:P, c * CHUNK : (c + 1) * CHUNK],
+                    )
+                tans.append(tan)
+
+        w2_grouped = keep.tile([P, N, PACK], BF16, name="w2_grouped", align_bytes=64)
+        nc.scalar.copy(w2_grouped[:], w2_raw[:].rearrange("p j c -> p c j"))
+        w2_scale = keep.tile([P, N], U8, name="w2_scale", align_bytes=64)
+
+        for half, groups in enumerate((((0, 1),), ((2,), (3,)))):
+            gain = keep.tile([P, PACK, HALF], F32, name="gain", tag="e_then_gain")
+            for t in range(PACK):
+                nc.vector.tensor_scalar(
+                    gain[:, t, :], squares[2 * half + t // 2][:, t % 2, :],
+                    minus_unit[:, t : t + 1], unit_sb[:, t : t + 1], ALU.mult, ALU.add,
+                )
+            zones = []
+            for group in groups:
+                zone = keep.tile([P, len(group), CHUNK, PACK], BF16, name="zone", tag="zone%d" % group[0], align_bytes=64)
+                for i, c in enumerate(group):
+                    part = c % 2
+                    nc.vector.tensor_tensor(
+                        zone[:, i], tans[c][:].rearrange("p t n -> p n t"),
+                        gain[:, :, part * CHUNK : (part + 1) * CHUNK].rearrange("p t n -> p n t"), ALU.mult,
+                    )
+                zones.append(zone)
+            accs = []
+            for group, zone in zip(groups, zones):
+                width = len(group) * CHUNK
+                zone_codes = keep.tile([P, width], U32, name="zone_codes%d" % group[0], align_bytes=64)
+                zone_scale = keep.tile([P, width], U8, name="zone_scale%d" % group[0], align_bytes=64)
+                nc.vector.quantize_mx(
+                    zone_codes[:].bitcast(FP8X4), zone_scale[:], zone[:].rearrange("p i n t -> p (i n t)")
+                )
+                if half == 0:
+                    w2_codes = keep.tile([P, N], U32, name="w2_codes", tag="zone0", align_bytes=64)
+                    nc.vector.quantize_mx(
+                        w2_codes[:].bitcast(FP8X4), w2_scale[:], w2_grouped[:].rearrange("p c j -> p (c j)")
+                    )
+                acc = psum.tile([P, width], F32, name="acc", tag="bank%d" % group[0])
+                nc.tensor.matmul_mx(
+                    acc[:], lhsT=w2_codes[:].bitcast(FP8X4), lhsT_scale=w2_scale[:],
+                    rhs=zone_codes[:].bitcast(FP8X4), rhs_scale=zone_scale[:], start=True, stop=True,
+                )
+                accs.append(acc)
+            for group, acc in zip(groups, accs):
+                width = len(group) * CHUNK
+                cols = slice(group[0] * CHUNK, group[0] * CHUNK + width)
+                result = keep.tile([P, width], F32, name="result%d" % group[0])
+                nc.vector.tensor_tensor(result[:], acc[:], skip_sb[:, cols], ALU.add)
+                nc.sync.dma_start(out[:, cols], result[:])

@@ -81,8 +81,8 @@ def tile_picked_yjvptn_jvp_p_kernel(
 
         def deal_w1(copy, a, m0, m1):
             copy(
-                w1_grouped[:, :, a * M_HALF + m0 : a * M_HALF + m1, :].rearrange("p t m j -> p m j t"),
-                w1_raw[a][:, :, PACK * m0 : PACK * m1].rearrange("p j (m t) -> p m j t", t=PACK),
+                w1_grouped[:, :, a * M_HALF + m0 : a * M_HALF + m1, :].rearrange("p (u v) m j -> p u m j v", v=2),
+                w1_raw[a][:, :, PACK * m0 : PACK * m1].rearrange("p j (m u v) -> p u m j v", u=2, v=2),
             )
 
         deal_w1(nc.scalar.copy, 0, 0, M_HALF)
@@ -136,7 +136,9 @@ def tile_picked_yjvptn_jvp_p_kernel(
                 tans.append(tan)
 
         w2_grouped = keep.tile([P, N, PACK], BF16, name="w2_grouped", align_bytes=64)
-        nc.scalar.copy(w2_grouped[:], w2_raw[:].rearrange("p j c -> p c j"))
+        nc.scalar.copy(
+            w2_grouped[:].rearrange("p (a b) j -> p a j b", b=2), w2_raw[:].rearrange("p j (a b) -> p a j b", b=2)
+        )
         w2_scale = keep.tile([P, N], U8, name="w2_scale", align_bytes=64)
 
         for half, groups in enumerate((((0, 1),), ((2,), (3,)))):
@@ -152,8 +154,10 @@ def tile_picked_yjvptn_jvp_p_kernel(
                 for i, c in enumerate(group):
                     part = c % 2
                     nc.vector.tensor_tensor(
-                        zone[:, i], tans[c][:].rearrange("p t n -> p n t"),
-                        gain[:, :, part * CHUNK : (part + 1) * CHUNK].rearrange("p t n -> p n t"), ALU.mult,
+                        zone[:, i].rearrange("p (a b) t -> p a t b", b=2),
+                        tans[c][:].rearrange("p t (a b) -> p a t b", b=2),
+                        gain[:, :, part * CHUNK : (part + 1) * CHUNK].rearrange("p t (a b) -> p a t b", b=2),
+                        ALU.mult,
                     )
                 zones.append(zone)
             accs = []

@@ -21,9 +21,7 @@ HALF = S // 2
 CHUNK = 128
 LIST_COLS = HALF // 16
 E_PLANE = 4
-W1_HALF = H // 2
-M_HALF = W1_HALF // PACK
-M_ON_SCALAR = 40
+M_ON_SCALAR = 96
 
 
 def tile_picked_yjvptn_jvp_p_kernel(
@@ -34,6 +32,8 @@ def tile_picked_yjvptn_jvp_p_kernel(
         keep = ctx.enter_context(tc.tile_pool(name="keep", bufs=1))
         psum = ctx.enter_context(tc.psum_pool(name="psum", bufs=1))
 
+        w1_raw = keep.tile([P, PACK, H], F32, name="w1_raw")
+        nc.sync.dma_start(w1_raw[:], w1.rearrange("(p j) c -> p j c", j=PACK))
         offsets = keep.tile([P, S // 16], U16, name="offsets")
         nc.sync.dma_start(offsets[:], offs)
 
@@ -56,15 +56,11 @@ def tile_picked_yjvptn_jvp_p_kernel(
 
         unit_sb = keep.tile([P, PACK], F32, name="unit_sb")
         nc.sync.dma_start(unit_sb[:], unit.rearrange("(p t) o -> p (t o)", t=PACK))
-        w1_rows = w1.rearrange("(p j) c -> p j c", j=PACK)
-        w1_raw = [keep.tile([P, PACK, W1_HALF], F32, name="w1_raw%d" % a) for a in range(2)]
-        nc.sync.dma_start(w1_raw[0][:], w1_rows[:, :, :W1_HALF])
         load_scale_rows(x_scale_table, x_scales, 0)
-        nc.sync.dma_start(w1_raw[1][:], w1_rows[:, :, W1_HALF:])
         x_table = keep.tile([P, T], U32, name="x_table")
         load_words(x_table, x_words)
         load_scale_rows(e_scale_table, e_scales, E_PLANE)
-        e_table = keep.tile([P, T], U32, name="e_table", tag="e_then_gain")
+        e_table = keep.tile([P, T], U32, name="e_table", tag="e_then_gain", align_bytes=64)
         load_words(e_table, e_words)
         w2_raw = keep.tile([P, PACK, N], F32, name="w2_raw")
         nc.sync.dma_start(w2_raw[:], w2.rearrange("(p j) c -> p j c", j=PACK))
@@ -79,15 +75,14 @@ def tile_picked_yjvptn_jvp_p_kernel(
 
         w1_grouped = keep.tile([P, PACK, P, PACK], BF16, name="w1_grouped", align_bytes=64)
 
-        def deal_w1(copy, a, m0, m1):
+        def deal_w1(copy, m0, m1):
             copy(
-                w1_grouped[:, :, a * M_HALF + m0 : a * M_HALF + m1, :].rearrange("p (u v) m j -> p u m j v", v=2),
-                w1_raw[a][:, :, PACK * m0 : PACK * m1].rearrange("p j (m u v) -> p u m j v", u=2, v=2),
+                w1_grouped[:, :, m0:m1, :].rearrange("p (u v) m j -> p u m j v", v=2),
+                w1_raw[:, :, PACK * m0 : PACK * m1].rearrange("p j (m u v) -> p u m j v", u=2, v=2),
             )
 
-        deal_w1(nc.scalar.copy, 0, 0, M_HALF)
-        deal_w1(nc.scalar.copy, 1, 0, M_ON_SCALAR)
-        deal_w1(nc.vector.tensor_copy, 1, M_ON_SCALAR, M_HALF)
+        deal_w1(nc.scalar.copy, 0, M_ON_SCALAR)
+        deal_w1(nc.vector.tensor_copy, M_ON_SCALAR, P)
         w1_codes = keep.tile([P, H], U32, name="w1_codes", tag="x_scale_then_w1", align_bytes=64)
         w1_scale = keep.tile([P, H], U8, name="w1_scale", align_bytes=64)
         nc.vector.quantize_mx(w1_codes[:].bitcast(FP8X4), w1_scale[:], w1_grouped[:].rearrange("p t m j -> p (t m j)"))
@@ -112,7 +107,7 @@ def tile_picked_yjvptn_jvp_p_kernel(
                     first_product(pre[:, i, :], 2 * pair + i, x_codes[:], x_scale[:, half * HALF : (half + 1) * HALF])
                 hid = keep.tile([P, 2, HALF], F32, name="hid", bufs=2)
                 nc.scalar.activation(hid[:], pre[:], ACT.Tanh)
-                square = keep.tile([P, 2, HALF], F32, name="square%d%d" % (half, pair))
+                square = keep.tile([P, 2, HALF], F32, name="square", tag="square%d%d" % (half, pair), align_bytes=64)
                 nc.scalar.activation(square[:], hid[:], ACT.Square)
                 squares.append(square)
 
@@ -135,40 +130,47 @@ def tile_picked_yjvptn_jvp_p_kernel(
                     )
                 tans.append(tan)
 
-        w2_grouped = keep.tile([P, N, PACK], BF16, name="w2_grouped", align_bytes=64)
-        nc.scalar.copy(
-            w2_grouped[:].rearrange("p (a b) j -> p a j b", b=2), w2_raw[:].rearrange("p j (a b) -> p a j b", b=2)
-        )
         w2_scale = keep.tile([P, N], U8, name="w2_scale", align_bytes=64)
 
+        gains = keep.tile([P, 2, PACK, HALF], F32, name="gains", tag="e_then_gain", align_bytes=64)
         for half, groups in enumerate((((0, 1),), ((2,), (3,)))):
-            gain = keep.tile([P, PACK, HALF], F32, name="gain", tag="e_then_gain")
+            gain = gains[:, half]
             for t in range(PACK):
-                nc.vector.tensor_scalar(
-                    gain[:, t, :], squares[2 * half + t // 2][:, t % 2, :],
-                    minus_unit[:, t : t + 1], unit_sb[:, t : t + 1], ALU.mult, ALU.add,
-                )
-            zones = []
-            for group in groups:
-                zone = keep.tile([P, len(group), CHUNK, PACK], BF16, name="zone", tag="zone%d" % group[0], align_bytes=64)
-                for i, c in enumerate(group):
-                    part = c % 2
-                    nc.vector.tensor_tensor(
-                        zone[:, i].rearrange("p (a b) t -> p a t b", b=2),
-                        tans[c][:].rearrange("p t (a b) -> p a t b", b=2),
-                        gain[:, :, part * CHUNK : (part + 1) * CHUNK].rearrange("p t (a b) -> p a t b", b=2),
-                        ALU.mult,
+                square = squares[2 * half + t // 2][:, t % 2, :]
+                if half == 1:
+                    nc.scalar.activation(
+                        gain[:, t, :], square, ACT.Identity, bias=unit_sb[:, t : t + 1], scale=minus_unit[:, t : t + 1]
                     )
-                zones.append(zone)
+                else:
+                    nc.vector.tensor_scalar(
+                        gain[:, t, :], square, minus_unit[:, t : t + 1], unit_sb[:, t : t + 1], ALU.mult, ALU.add
+                    )
+            zone = keep.tile(
+                [P, 2, CHUNK, PACK], BF16, name="zone", tag="zone0" if half == 0 else "square01", align_bytes=64
+            )
+            for part in range(2):
+                nc.vector.tensor_tensor(
+                    zone[:, part].rearrange("p (a b) t -> p a t b", b=2),
+                    tans[2 * half + part][:].rearrange("p t (a b) -> p a t b", b=2),
+                    gain[:, :, part * CHUNK : (part + 1) * CHUNK].rearrange("p t (a b) -> p a t b", b=2),
+                    ALU.mult,
+                )
             accs = []
-            for group, zone in zip(groups, zones):
+            for group in groups:
                 width = len(group) * CHUNK
                 zone_codes = keep.tile([P, width], U32, name="zone_codes%d" % group[0], align_bytes=64)
                 zone_scale = keep.tile([P, width], U8, name="zone_scale%d" % group[0], align_bytes=64)
                 nc.vector.quantize_mx(
-                    zone_codes[:].bitcast(FP8X4), zone_scale[:], zone[:].rearrange("p i n t -> p (i n t)")
+                    zone_codes[:].bitcast(FP8X4), zone_scale[:],
+                    zone[:, group[0] % 2 : group[-1] % 2 + 1].rearrange("p i n t -> p (i n t)"),
                 )
                 if half == 0:
+                    w2_grouped = keep.tile([P, N, PACK], BF16, name="w2_grouped", tag="square01", align_bytes=64)
+                    nc.gpsimd.tensor_scalar(
+                        w2_grouped[:].rearrange("p (a b) j -> p a j b", b=2),
+                        w2_raw[:].rearrange("p j (a b) -> p a j b", b=2),
+                        1.0, 0.0, ALU.mult, ALU.add,
+                    )
                     w2_codes = keep.tile([P, N], U32, name="w2_codes", tag="zone0", align_bytes=64)
                     nc.vector.quantize_mx(
                         w2_codes[:].bitcast(FP8X4), w2_scale[:], w2_grouped[:].rearrange("p c j -> p (c j)")

@@ -146,7 +146,7 @@ def tile_picked_yjvptn_jvp_p_kernel(
                         gain[:, t, :], square, minus_unit[:, t : t + 1], unit_sb[:, t : t + 1], ALU.mult, ALU.add
                     )
             zone = keep.tile(
-                [P, 2, CHUNK, PACK], BF16, name="zone", tag="zone0" if half == 0 else "square01", align_bytes=64
+                [P, 2, CHUNK, PACK], BF16, name="zone", align_bytes=64
             )
             for part in range(2):
                 nc.vector.tensor_tensor(
@@ -155,26 +155,24 @@ def tile_picked_yjvptn_jvp_p_kernel(
                     gain[:, :, part * CHUNK : (part + 1) * CHUNK].rearrange("p t (a b) -> p a t b", b=2),
                     ALU.mult,
                 )
+            if half == 0:
+                w2_grouped = keep.tile([P, N, PACK], BF16, name="w2_grouped", tag="square01", align_bytes=64)
+                nc.gpsimd.tensor_scalar(
+                    w2_grouped[:], w2_raw[:].rearrange("p j c -> p c j"), 1.0, 0.0, ALU.mult, ALU.add
+                )
+                w2_codes = keep.tile([P, N], U32, name="w2_codes", align_bytes=64)
+                nc.vector.quantize_mx(
+                    w2_codes[:].bitcast(FP8X4), w2_scale[:], w2_grouped[:].rearrange("p c j -> p (c j)")
+                )
             accs = []
             for group in groups:
                 width = len(group) * CHUNK
-                zone_codes = keep.tile([P, width], U32, name="zone_codes%d" % group[0], align_bytes=64)
+                zone_codes = keep.tile([P, width], U32, name="zone_codes", tag="square01" if half == 0 else "zone_codes%d" % group[0], align_bytes=64)
                 zone_scale = keep.tile([P, width], U8, name="zone_scale%d" % group[0], align_bytes=64)
                 nc.vector.quantize_mx(
                     zone_codes[:].bitcast(FP8X4), zone_scale[:],
                     zone[:, group[0] % 2 : group[-1] % 2 + 1].rearrange("p i n t -> p (i n t)"),
                 )
-                if half == 0:
-                    w2_grouped = keep.tile([P, N, PACK], BF16, name="w2_grouped", tag="square01", align_bytes=64)
-                    nc.gpsimd.tensor_scalar(
-                        w2_grouped[:].rearrange("p (a b) j -> p a j b", b=2),
-                        w2_raw[:].rearrange("p j (a b) -> p a j b", b=2),
-                        1.0, 0.0, ALU.mult, ALU.add,
-                    )
-                    w2_codes = keep.tile([P, N], U32, name="w2_codes", tag="zone0", align_bytes=64)
-                    nc.vector.quantize_mx(
-                        w2_codes[:].bitcast(FP8X4), w2_scale[:], w2_grouped[:].rearrange("p c j -> p (c j)")
-                    )
                 acc = psum.tile([P, width], F32, name="acc", tag="bank%d" % group[0])
                 nc.tensor.matmul_mx(
                     acc[:], lhsT=w2_codes[:].bitcast(FP8X4), lhsT_scale=w2_scale[:],
@@ -185,5 +183,10 @@ def tile_picked_yjvptn_jvp_p_kernel(
                 width = len(group) * CHUNK
                 cols = slice(group[0] * CHUNK, group[0] * CHUNK + width)
                 result = keep.tile([P, width], F32, name="result%d" % group[0])
-                nc.vector.tensor_tensor(result[:], acc[:], skip_sb[:, cols], ALU.add)
+                if half == 0:
+                    product = keep.tile([P, width], F32, name="product")
+                    nc.scalar.copy(product[:], acc[:])
+                    nc.gpsimd.tensor_tensor(result[:], product[:], skip_sb[:, cols], ALU.add)
+                else:
+                    nc.vector.tensor_tensor(result[:], acc[:], skip_sb[:, cols], ALU.add)
                 nc.sync.dma_start(out[:, cols], result[:])

from contextlib import ExitStack

import concourse.mybir as mybir

H, K, T, S, N = 512, 512, 2048, 512, 128
FLOPS = 2 * K * H * S * 2 + 2 * H * N * S

F32 = mybir.dt.float32
BF16 = mybir.dt.bfloat16
I32 = mybir.dt.int32
U32 = mybir.dt.uint32
U16 = mybir.dt.uint16
U8 = mybir.dt.uint8
FP8X4 = mybir.dt.float8_e4m3fn_x4
ACT = mybir.ActivationFunctionType
ALU = mybir.AluOpType

P = 128
PACK = 4
HALF = S // 2
CHUNK = 128
LIST_COLS = HALF // 16
E_PLANE = 4
M_ON_SCALAR = 96


def tile_picked_yjvptn_jvp_p_kernel(
    tc, x_words, x_scales, e_words, e_scales, w1, unit, w2, skip, offs, out
):
    nc = tc.nc
    with ExitStack() as ctx:
        keep = ctx.enter_context(tc.tile_pool(name="keep", bufs=1))
        psum = ctx.enter_context(tc.psum_pool(name="psum", bufs=1))

        w1_raw = keep.tile([P, PACK, H], F32, name="w1_raw")
        nc.sync.dma_start(w1_raw[:], w1.rearrange("(p j) c -> p j c", j=PACK))
        offsets = keep.tile([P, S // 16], U16, name="offsets")
        nc.sync.dma_start(offsets[:], offs)

        x_scale_table = keep.tile([P, T], U8, name="x_scale_table", tag="x_scale_then_w1", align_bytes=64)
        e_scale_table = keep.tile([P, T], U8, name="e_scale_table", tag="e_scale_then_codes", align_bytes=64)
        nc.vector.memset(x_scale_table[:].bitcast(I32), 0)
        nc.vector.memset(e_scale_table[:].bitcast(I32), 0)

        warm_in = keep.tile([P, 1], F32, name="warm_in")
        warm_out = keep.tile([P, 1], F32, name="warm_out")
        nc.gpsimd.memset(warm_in[:], 0.0)
        nc.scalar.activation(warm_out[:], warm_in[:], ACT.Tanh)

        def load_scale_rows(table, scales, plane):
            for r in range(4):
                nc.sync.dma_start(table[plane + r : P : 32, :].bitcast(I32), scales[0, r:16:4, :].bitcast(I32))

        def load_words(table, words):
            nc.sync.dma_start(table[:].bitcast(I32), words[0].rearrange("p n t -> p (n t)").bitcast(I32))

        unit_sb = keep.tile([P, PACK], F32, name="unit_sb")
        nc.sync.dma_start(unit_sb[:], unit.rearrange("(p t) o -> p (t o)", t=PACK))
        load_scale_rows(x_scale_table, x_scales, 0)
        x_table = keep.tile([P, T], U32, name="x_table")
        load_words(x_table, x_words)
        load_scale_rows(e_scale_table, e_scales, E_PLANE)
        e_table = keep.tile([P, T], U32, name="e_table", tag="e_then_gain", align_bytes=64)
        load_words(e_table, e_words)
        w2_raw = keep.tile([P, PACK, N], F32, name="w2_raw")
        nc.sync.dma_start(w2_raw[:], w2.rearrange("(p j) c -> p j c", j=PACK))
        skip_sb = keep.tile([P, S], F32, name="skip_sb")
        nc.sync.dma_start(skip_sb[:], skip)

        x_scale = keep.tile([P, S], U8, name="x_scale", align_bytes=64)
        nc.vector.tensor_copy(x_scale[:], x_scale_table[:].indirect(offsets[:]))

        minus_unit = keep.tile([P, PACK], F32, name="minus_unit")
        nc.vector.tensor_scalar(minus_unit[:], unit_sb[:], -1.0, None, ALU.mult)

        w1_grouped = keep.tile([P, PACK, P, PACK], BF16, name="w1_grouped", align_bytes=64)

        def deal_w1(copy, m0, m1):
            copy(
                w1_grouped[:, :, m0:m1, :].rearrange("p (u v) m j -> p u m j v", v=2),
                w1_raw[:, :, PACK * m0 : PACK * m1].rearrange("p j (m u v) -> p u m j v", u=2, v=2),
            )

        deal_w1(nc.scalar.copy, 0, M_ON_SCALAR)
        deal_w1(nc.vector.tensor_copy, M_ON_SCALAR, P)
        w1_codes = keep.tile([P, H], U32, name="w1_codes", tag="x_scale_then_w1", align_bytes=64)
        w1_scale = keep.tile([P, H], U8, name="w1_scale", align_bytes=64)
        nc.vector.quantize_mx(w1_codes[:].bitcast(FP8X4), w1_scale[:], w1_grouped[:].rearrange("p t m j -> p (t m j)"))

        def first_product(bank, t, codes, scale):
            cols = slice(t * P, (t + 1) * P)
            nc.tensor.matmul_mx(
                bank, lhsT=w1_codes[:, cols].bitcast(FP8X4), lhsT_scale=w1_scale[:, cols],
                rhs=codes.bitcast(FP8X4), rhs_scale=scale, start=True, stop=True,
            )

        def list_half(half):
            return offsets[:, half * LIST_COLS : (half + 1) * LIST_COLS]

        squares = []
        for half in range(2):
            x_codes = keep.tile([P, HALF], U32, name="x_codes%d" % half, align_bytes=64)
            nc.vector.tensor_copy(x_codes[:], x_table[:].indirect(list_half(half)))
            for pair in range(2):
                pre = psum.tile([P, 2, HALF], F32, name="pre", tag="bank%d" % (2 * half + pair))
                for i in range(2):
                    first_product(pre[:, i, :], 2 * pair + i, x_codes[:], x_scale[:, half * HALF : (half + 1) * HALF])
                hid = keep.tile([P, 2, HALF], F32, name="hid", bufs=2)
                nc.scalar.activation(hid[:], pre[:], ACT.Tanh)
                square = keep.tile([P, 2, HALF], F32, name="square", tag="square%d%d" % (half, pair), align_bytes=64)
                nc.scalar.activation(square[:], hid[:], ACT.Square)
                squares.append(square)

        e_scale = keep.tile([P, S], U8, name="e_scale", align_bytes=64)
        nc.vector.tensor_copy(e_scale[:], e_scale_table[:].indirect(offsets[:]))

        tans = []
        for half in range(2):
            e_codes = keep.tile(
                [P, HALF], U32, name="e_codes", tag="e_scale_then_codes" if half == 0 else "e_codes", align_bytes=64
            )
            nc.vector.tensor_copy(e_codes[:], e_table[:].indirect(list_half(half)))
            for part in range(2):
                c = 2 * half + part
                tan = psum.tile([P, PACK, CHUNK], F32, name="tan", tag="bank%d" % (4 + c))
                for t in range(PACK):
                    first_product(
                        tan[:, t, :], t, e_codes[:, part * CHUNK : (part + 1) * CHUNK],
                        e_scale[E_PLANE:P, c * CHUNK : (c + 1) * CHUNK],
                    )
                tans.append(tan)

        w2_scale = keep.tile([P, N], U8, name="w2_scale", align_bytes=64)

        gains = keep.tile([P, 2, PACK, HALF], F32, name="gains", tag="e_then_gain", align_bytes=64)
        for half, groups in enumerate((((0, 1),), ((2,), (3,)))):
            gain = gains[:, half]
            for t in range(PACK):
                square = squares[2 * half + t // 2][:, t % 2, :]
                if half == 1:
                    nc.scalar.activation(
                        gain[:, t, :], square, ACT.Identity, bias=unit_sb[:, t : t + 1], scale=minus_unit[:, t : t + 1]
                    )
                else:
                    nc.vector.tensor_scalar(
                        gain[:, t, :], square, minus_unit[:, t : t + 1], unit_sb[:, t : t + 1], ALU.mult, ALU.add
                    )
            zone = keep.tile(
                [P, 2, CHUNK, PACK], BF16, name="zone", align_bytes=64
            )
            for part in range(2):
                nc.vector.tensor_tensor(
                    zone[:, part].rearrange("p (a b) t -> p a t b", b=2),
                    tans[2 * half + part][:].rearrange("p t (a b) -> p a t b", b=2),
                    gain[:, :, part * CHUNK : (part + 1) * CHUNK].rearrange("p t (a b) -> p a t b", b=2),
                    ALU.mult,
                )
            if half == 0:
                w2_grouped = keep.tile([P, N, PACK], BF16, name="w2_grouped", tag="square01", align_bytes=64)
                nc.gpsimd.tensor_scalar(
                    w2_grouped[:], w2_raw[:].rearrange("p j c -> p c j"), 1.0, 0.0, ALU.mult, ALU.add
                )
                w2_codes = keep.tile([P, N], U32, name="w2_codes", align_bytes=64)
                nc.vector.quantize_mx(
                    w2_codes[:].bitcast(FP8X4), w2_scale[:], w2_grouped[:].rearrange("p c j -> p (c j)")
                )
            accs = []
            for group in groups:
                width = len(group) * CHUNK
                zone_codes = keep.tile([P, width], U32, name="zone_codes", tag="square01" if half == 0 else "zone_codes%d" % group[0], align_bytes=64)
                zone_scale = keep.tile([P, width], U8, name="zone_scale%d" % group[0], align_bytes=64)
                nc.vector.quantize_mx(
                    zone_codes[:].bitcast(FP8X4), zone_scale[:],
                    zone[:, group[0] % 2 : group[-1] % 2 + 1].rearrange("p i n t -> p (i n t)"),
                )
                acc = psum.tile([P, width], F32, name="acc", tag="bank%d" % group[0])
                nc.tensor.matmul_mx(
                    acc[:], lhsT=w2_codes[:].bitcast(FP8X4), lhsT_scale=w2_scale[:],
                    rhs=zone_codes[:].bitcast(FP8X4), rhs_scale=zone_scale[:], start=True, stop=True,
                )
                accs.append(acc)
            for group, acc in zip(groups, accs):
                width = len(group) * CHUNK
                cols = slice(group[0] * CHUNK, group[0] * CHUNK + width)
                result = keep.tile([P, width], F32, name="result%d" % group[0])
                if half == 0:
                    product = keep.tile([P, width], F32, name="product")
                    nc.scalar.copy(product[:], acc[:])
                    nc.gpsimd.tensor_tensor(result[:], product[:], skip_sb[:, cols], ALU.add)
                else:
                    nc.vector.tensor_tensor(result[:], acc[:], skip_sb[:, cols], ALU.add)
                nc.sync.dma_start(out[:, cols], result[:])
